import numpy as np, ml_dtypes
CORES = [1,3,5,9,11,13]
N = 6
import mx_ref
NC, G = 384, 4
C = np.float32(0.019)
BF = ml_dtypes.bfloat16
def cut(t, i, w=512):
    return t[:, w * i:w * i + w]
def tile(rs):
    return np.stack(rs, axis=2).reshape(128, -1).astype(BF)
def layer(w, X):
    out = []
    for i in range(G):
        for t in range(len(X)):
            p = mx_ref.matmul(mx_ref.quantize(cut(w, len(X) * i + t)), X[t])
            z = p if t == 0 else z + p
        out.append(z)
    return out
def rot(Z, c, s):
    return [(Z[0] * c - Z[1] * s) * C, (Z[0] * s + Z[1] * c) * C, (Z[2] * c - Z[3] * s) * C, (Z[2] * s + Z[3] * c) * C]
def setup_inputs(rng):
    def f(*shape):
        return mx_ref.flush((rng.standard_normal(shape, dtype=np.float32) * np.exp2(rng.integers(-2, 3, shape[:-1] + (1,)))).astype(BF))
    ang = rng.random((N, 128, 128)) * (2 * np.pi)
    return {"cs": np.cos(ang).astype(BF), "sn": np.sin(ang).astype(BF), "xk": f(N, 128, 512), "wk": f(N, 128, G * 512), "xq": f(N, 128, 4 * NC)}
def setup_inputs_blocks(rng):
    d = setup_inputs(rng)
    for k in ("xk", "wk", "xq"): d[k] = mx_ref.spread(d[k], rng, 4)
    return d
def setup_inputs_wide(rng):
    d = setup_inputs(rng)
    for k in ("xk", "wk", "xq"): d[k] = mx_ref.flush((d[k].astype(np.float32) * np.exp2(rng.integers(-5, 6, (N, 1, 1))).astype(np.float32)).astype(BF))
    return d
def setup_inputs_zeros(rng):
    d = setup_inputs(rng); v = d["xk"].reshape(N, 128, -1, 4).copy()
    v[np.broadcast_to((rng.random((N, 1, v.shape[2], 1)) < 0.33), v.shape)] = 0
    d["xk"] = v.reshape(d["xk"].shape)
    return d
def reference(cs, sn, xk, wk, xq):
    K = [mx_ref.quantize(tile(rot(layer(wk[j], [mx_ref.quantize(xk[j])]), cs[j].astype(np.float32), sn[j].astype(np.float32)))) for j in range(N)]
    y = np.zeros((N, 128, N * NC), np.float32)
    for r in range(N):
        q = mx_ref.quantize(xq[r])
        for j in range(N):
            y[r][:, NC * j:NC * j + NC] = mx_ref.matmul(K[j], q)
    return {"y": y}

@@ -1,0 +1,239 @@
+from concourse.bass import DstId, RemoteDMATransfer
+from concourse.mybir import dt, AluOpType, ActivationFunctionType
+
+N = 6
+NQ = 384
+H = NQ // 2
+SIM_CORES = 16
+
+SCRATCH = {
+    "xks": ("sbuf", [128, 512], "bfloat16"),
+    "wks": ("sbuf", [128, 2048], "bfloat16"),
+    "xqs": ("sbuf", [128, 4 * NQ], "bfloat16"),
+    "css": ("sbuf", [128, 128], "bfloat16"),
+    "sns": ("sbuf", [128, 128], "bfloat16"),
+    "xc": ("sbuf", [128, 128], "float8_e4m3fn_x4"),
+    "xp": ("sbuf", [128, 128], "uint8"),
+    "wc": ("sbuf", [128, 512], "float8_e4m3fn_x4"),
+    "wp": ("sbuf", [128, 512], "uint8"),
+    "qc": ("sbuf", [128, NQ], "float8_e4m3fn_x4"),
+    "qp": ("sbuf", [128, NQ], "uint8"),
+    "kc": ("sbuf", [128, N * 128], "float8_e4m3fn_x4"),
+    "kp": ("sbuf", [128, N * 128], "uint8"),
+    "rot": ("sbuf", [128, 512], "bfloat16"),
+    "da": ("sbuf", [128, 512], "float32"),
+    "db": ("sbuf", [128, 512], "float32"),
+    "ra": ("sbuf", [128, 512], "float32"),
+    "rb": ("sbuf", [128, 512], "float32"),
+    "kt": ("sbuf", [128, 512], "bfloat16"),
+    "ys": ("sbuf", [128, N * NQ], "float32"),
+    "ps": ("psum", [128, 4096], "float32"),
+}
+SEMAPHORES = (
+    ["l_xk", "l_wa", "l_wb", "l_cs", "l_sn", "l_xq", "zero", "da", "db0", "db1", "sa", "sb0", "sb1", "tk", "qk", "qq",
+     "qx", "rc", "rp", "inx", "sent", "st"]
+    + ["qw%d" % i for i in range(4)] + ["z%d" % i for i in range(4)] + ["in%d" % i for i in range(N)]
+    + ["p%d_%d" % (i, h) for i in range(N) for h in range(2)] + ["e%d_%d" % (i, h) for i in range(N) for h in range(2)])
+
+
+def bits(mask):
+    return bin(mask).count("1")
+
+
+def plan(T, topo):
+    cores = list(T.cores)
+    chips = sorted(set(topo.chip(c) for c in cores))
+    direct, indirect, relay = {}, {}, {}
+    for ch in chips:
+        here = [c for c in cores if topo.chip(c) == ch]
+        far = [c for c in cores if topo.chip(c) != ch]
+        direct[ch] = [c for c in here if all(topo.may_write(c, f) for f in far)]
+        indirect[ch] = [c for c in here if c not in direct[ch]]
+        free = [c for c in range(SIM_CORES) if topo.chip(c) == ch and c not in cores
+                and all(topo.may_write(c, f) for f in far)]
+        for same in (True, False):
+            for f in far:
+                if f in relay:
+                    continue
+                fit = [c for c in free if not same or topo.die(c) == topo.die(f)]
+                if fit:
+                    relay[f] = fit[0]
+                    free.remove(fit[0])
+    order = [c for ch in chips for c in indirect[ch]] + [c for ch in chips for c in direct[ch]]
+    slot = {c: i for i, c in enumerate(order)}
+    return direct, indirect, relay, slot
+
+
+def rank_program(g, core, T, topo):
+    S = T.sem
+    rank = T.rank_of(core)
+    cores = list(T.cores)
+    mychip = topo.chip(core)
+    direct, indirect, relay, slot = plan(T, topo)
+    mates = [c for c in cores if topo.chip(c) == mychip and c != core]
+    far = [c for c in cores if topo.chip(c) != mychip]
+
+    def codes(s, n=1):
+        return T.kc[:, 128 * s:128 * (s + n)].bitcast(dt.uint8)
+
+    def planes(s, n=1):
+        return T.kp[:, 128 * s:128 * (s + n)]
+
+    def put(view, dsts, mask, sem):
+        ids = []
+        for d in dsts:
+            rid, pid, _ = topo.addr(d)
+            ids.append(DstId(rid=rid, pnc=pid))
+        return RemoteDMATransfer(dst_ids=ids, dma_engine_mask=mask, remote_sem=sem, srcs=[view], dsts=[view] * len(ids))
+
+    def common(src, dsts):
+        m = topo.mask(src, dsts[0])
+        for d in dsts[1:]:
+            m &= topo.mask(src, d)
+        return m
+
+    def here_mask(src):
+        ms = [c for c in cores if topo.chip(c) == topo.chip(src) and c != src]
+        m = common(src, ms)
+        if src in direct[topo.chip(src)]:
+            m &= ~common(src, [c for c in cores if topo.chip(c) != topo.chip(src)])
+        return m
+
+    if rank is None:
+        mine = [f for f in relay if relay[f] == core]
+        if not mine:
+            return
+        f = mine[0]
+        src = indirect[mychip]
+        s, n = slot[src[0]], len(src)
+        arr = sum(bits(topo.mask(c, core)) for c in src)
+        m = topo.mask(core, f)
+        g.wait_ge(S.rc, arr)
+        g.remote_dma_fused([put(codes(s, n), [f], m, S.inx)], local_sem=S.sent)
+        g.wait_ge(S.rp, arr)
+        g.remote_dma_fused([put(planes(s, n), [f], m, S.inx)], local_sem=S.sent)
+        g.wait_ge(S.sent, 2 * bits(m))
+        return
+
+    v, sc, te, sy = g.vector, g.scalar, g.tensor, g.sync
+    mult, add = AluOpType.mult, AluOpType.add
+    Copy = ActivationFunctionType.Copy
+    K = 0.019
+    me = slot[core]
+
+    sy.dma_start(T.xks[:], T.xk[:]).then_inc(S.l_xk, 16)
+    sc.dma_start(T.wks[:, 0:1024], T.wk[:, 0:1024]).then_inc(S.l_wa, 16)
+    sy.dma_start(T.css[:], T.cs[:]).then_inc(S.l_cs, 16)
+    sc.dma_start(T.sns[:], T.sn[:]).then_inc(S.l_sn, 16)
+    sy.dma_start(T.wks[:, 1024:2048], T.wk[:, 1024:2048]).then_inc(S.l_wb, 16)
+    sy.dma_start(T.xqs[:], T.xq[:]).then_inc(S.l_xq, 16)
+
+    def zb(i):
+        return T.ps[:, 512 * i:512 * i + 128]
+
+    def qw(i):
+        a = 128 * i
+        v.quantize_mx(T.wc[:, a:a + 128], T.wp[:, a:a + 128], T.wks[:, 4 * a:4 * a + 512]).then_inc(S["qw%d" % i], 1)
+
+    te.wait_ge(S.qx, 1)
+    for i in range(4):
+        a = 128 * i
+        te.wait_ge(S["qw%d" % i], 1)
+        te.matmul_mx(zb(i), T.wc[:, a:a + 128], T.wp[:, a:a + 128], T.xc[:], T.xp[:], True, True).then_inc(S["z%d" % i], 1)
+
+    v.memset(T.rot[:], 0.0).then_inc(S.zero, 1)
+    v.wait_ge(S.l_xk, 16)
+    v.quantize_mx(T.xc[:], T.xp[:], T.xks[:]).then_inc(S.qx, 1)
+    v.wait_ge(S.l_wa, 16)
+    qw(0)
+    qw(1)
+    v.wait_ge(S.l_cs, 16)
+    v.wait_ge(S.l_sn, 16)
+    v.wait_ge(S.z0, 1)
+    v.tensor_tensor(T.da[:, 1:256:2], zb(0), T.css[:], mult).then_inc(S.da, 1)
+    v.tensor_tensor(T.da[:, 257:512:2], zb(0), T.sns[:], mult).then_inc(S.da, 1)
+    v.wait_ge(S.da, 6)
+    v.tensor_tensor_scan(T.ra[:], T.rot[:], T.da[:], 0.0, mult, add).then_inc(S.sa, 1)
+    v.wait_ge(S.l_wb, 16)
+    qw(2)
+    qw(3)
+    v.wait_ge(S.z2, 1)
+    v.tensor_tensor(T.db[:, 1:256:2], zb(2), T.css[:], mult).then_inc(S.db0, 1)
+    v.tensor_tensor(T.db[:, 257:512:2], zb(2), T.sns[:], mult).then_inc(S.db1, 1)
+    v.wait_ge(S.db0, 2)
+    v.tensor_tensor_scan(T.rb[:, 0:256], T.rot[:, 0:256], T.db[:, 0:256], 0.0, mult, add).then_inc(S.sb0, 1)
+    v.wait_ge(S.db1, 2)
+    v.tensor_tensor_scan(T.rb[:, 256:512], T.rot[:, 256:512], T.db[:, 256:512], 0.0, mult, add).then_inc(S.sb1, 1)
+    v.wait_ge(S.sb1, 1)
+    v.tensor_scalar(T.kt[:, 3:512:4], T.rb[:, 257:512:2], K, None, mult).then_inc(S.tk, 1)
+    v.wait_ge(S.tk, 4)
+    v.quantize_mx(T.kc[:, 128 * me:128 * me + 128], T.kp[:, 128 * me:128 * me + 128], T.kt[:]).then_inc(S.qk, 1)
+    v.wait_ge(S.l_xq, 16)
+    v.quantize_mx(T.qc[:], T.qp[:], T.xqs[:]).then_inc(S.qq, 1)
+
+    sc.wait_ge(S.zero, 1)
+    sc.wait_ge(S.l_cs, 16)
+    sc.activation(T.rot[:, 257:512:2], T.css[:], Copy).then_inc(S.da, 1)
+    sc.wait_ge(S.l_sn, 16)
+    sc.activation(T.rot[:, 1:256:2], T.sns[:], Copy, scale=-1.0).then_inc(S.da, 1)
+    sc.wait_ge(S.z1, 1)
+    sc.activation(T.da[:, 0:256:2], zb(1), Copy).then_inc(S.da, 1)
+    sc.activation(T.da[:, 256:512:2], zb(1), Copy).then_inc(S.da, 1)
+    sc.wait_ge(S.sa, 1)
+    sc.activation(T.kt[:, 0:512:4], T.ra[:, 1:256:2], Copy, scale=K).then_inc(S.tk, 1)
+    sc.activation(T.kt[:, 1:512:4], T.ra[:, 257:512:2], Copy, scale=K).then_inc(S.tk, 1)
+    sc.wait_ge(S.z3, 1)
+    sc.activation(T.db[:, 0:256:2], zb(3), Copy).then_inc(S.db0, 1)
+    sc.activation(T.db[:, 256:512:2], zb(3), Copy).then_inc(S.db1, 1)
+    sc.wait_ge(S.sb0, 1)
+    sc.activation(T.kt[:, 2:512:4], T.rb[:, 1:256:2], Copy, scale=K).then_inc(S.tk, 1)
+
+    g.wait_ge(S.qk, 1)
+    arrive = S["in%d" % me]
+    mh = here_mask(core)
+    if core in direct[mychip]:
+        mf = common(core, far)
+        for part in (codes(me), planes(me)):
+            g.remote_dma_fused([put(part, far, mf, arrive), put(part, mates, mh, arrive)], local_sem=S.sent)
+        sent = 2 * (bits(mf) + bits(mh))
+    else:
+        via = [relay[f] for f in far]
+        mr = common(core, via)
+        g.remote_dma_fused([put(codes(me), via, mr, S.rc)], local_sem=S.sent)
+        g.remote_dma_fused([put(planes(me), via, mr, S.rp)], local_sem=S.sent)
+        g.remote_dma_fused([put(codes(me), mates, mh, arrive)], local_sem=S.sent)
+        g.remote_dma_fused([put(planes(me), mates, mh, arrive)], local_sem=S.sent)
+        sent = 2 * (bits(mr) + bits(mh))
+    g.wait_ge(S.sent, sent)
+
+    farchip = topo.chip(far[0])
+    order = [(core, None, 0)]
+    for c in sorted(mates, key=lambda c: c not in direct[mychip]):
+        order.append((c, S["in%d" % slot[c]], 2 * bits(here_mask(c))))
+    for c in direct[farchip]:
+        order.append((c, S["in%d" % slot[c]], 2 * bits(common(c, [core] + mates))))
+    for c in indirect[farchip]:
+        order.append((c, S.inx, 2 * bits(topo.mask(relay[core], core))))
+    for i, (c, sem, cnt) in enumerate(order):
+        j = cores.index(c)
+        s = slot[c]
+        banks = [512 * ((4 + 2 * i + h) % 8) for h in range(2)]
+        if i == 0:
+            te.wait_ge(S.qk, 1)
+            te.wait_ge(S.qq, 1)
+        else:
+            te.wait_ge(sem, cnt)
+        for h in range(2):
+            if i >= 4:
+                te.wait_ge(S["e%d_%d" % (i - 4, h)], 1)
+            te.matmul_mx(T.ps[:, banks[h]:banks[h] + H], T.kc[:, 128 * s:128 * s + 128], T.kp[:, 128 * s:128 * s + 128],
+                         T.qc[:, H * h:H * h + H], T.qp[:, H * h:H * h + H], True, True).then_inc(S["p%d_%d" % (i, h)], 1)
+        a = NQ * j
+        v.wait_ge(S["p%d_0" % i], 1)
+        v.tensor_copy(T.ys[:, a:a + H], T.ps[:, banks[0]:banks[0] + H]).then_inc(S["e%d_0" % i], 1)
+        sc.wait_ge(S["p%d_1" % i], 1)
+        sc.activation(T.ys[:, a + H:a + NQ], T.ps[:, banks[1]:banks[1] + H], Copy).then_inc(S["e%d_1" % i], 1)
+        sy.wait_ge(S["e%d_0" % i], 1)
+        sy.wait_ge(S["e%d_1" % i], 1)
+        sy.dma_start(T.y[:, a:a + NQ], T.ys[:, a:a + NQ]).then_inc(S.st, 16)
+    sy.wait_ge(S.st, 16 * N)

@@ -3,8 +3,9 @@ from concourse.mybir import dt, AluOpType, ActivationFunctionType
 
 N = 6
 NQ = 384
-H = NQ // 2
+CUTS = ((0, 256), (256, 384))
 SIM_CORES = 16
+E_HOP1 = 8
 
 SCRATCH = {
     "xks": ("sbuf", [128, 512], "bfloat16"),
@@ -40,10 +41,16 @@ def bits(mask):
     return bin(mask).count("1")
 
 
+def some(mask, n, part=0):
+    e = [i for i in range(mask.bit_length()) if mask >> i & 1]
+    k = part * n % len(e)
+    return sum(1 << i for i in e[k:k + n])
+
+
 def plan(T, topo):
     cores = list(T.cores)
     chips = sorted(set(topo.chip(c) for c in cores))
-    direct, indirect, relay = {}, {}, {}
+    direct, indirect, crelay, prelay = {}, {}, {}, {}
     for ch in chips:
         here = [c for c in cores if topo.chip(c) == ch]
         far = [c for c in cores if topo.chip(c) != ch]
@@ -51,17 +58,13 @@ def plan(T, topo):
         indirect[ch] = [c for c in here if c not in direct[ch]]
         free = [c for c in range(SIM_CORES) if topo.chip(c) == ch and c not in cores
                 and all(topo.may_write(c, f) for f in far)]
-        for same in (True, False):
-            for f in far:
-                if f in relay:
-                    continue
-                fit = [c for c in free if not same or topo.die(c) == topo.die(f)]
-                if fit:
-                    relay[f] = fit[0]
-                    free.remove(fit[0])
+        for c in indirect[ch]:
+            crelay[c] = sorted(free, key=lambda r: (topo.die(r) != topo.die(c), r))[0]
+            free.remove(crelay[c])
+        prelay[ch] = free[0]
     order = [c for ch in chips for c in indirect[ch]] + [c for ch in chips for c in direct[ch]]
     slot = {c: i for i, c in enumerate(order)}
-    return direct, indirect, relay, slot
+    return direct, indirect, crelay, prelay, slot
 
 
 def rank_program(g, core, T, topo):
@@ -69,12 +72,12 @@ def rank_program(g, core, T, topo):
     rank = T.rank_of(core)
     cores = list(T.cores)
     mychip = topo.chip(core)
-    direct, indirect, relay, slot = plan(T, topo)
+    direct, indirect, crelay, prelay, slot = plan(T, topo)
     mates = [c for c in cores if topo.chip(c) == mychip and c != core]
     far = [c for c in cores if topo.chip(c) != mychip]
 
-    def codes(s, n=1):
-        return T.kc[:, 128 * s:128 * (s + n)].bitcast(dt.uint8)
+    def codes(s):
+        return T.kc[:, 128 * s:128 * (s + 1)].bitcast(dt.uint8)
 
     def planes(s, n=1):
         return T.kp[:, 128 * s:128 * (s + n)]
@@ -99,20 +102,25 @@ def rank_program(g, core, T, topo):
             m &= ~common(src, [c for c in cores if topo.chip(c) != topo.chip(src)])
         return m
 
+    def far_order(relay):
+        fs = [c for c in cores if topo.chip(c) != topo.chip(relay)]
+        fs = sorted(fs, key=lambda f: -topo.die(f))
+        return fs if topo.die(relay) == topo.die(fs[0]) else fs[::-1]
+
     if rank is None:
-        mine = [f for f in relay if relay[f] == core]
-        if not mine:
-            return
-        f = mine[0]
-        src = indirect[mychip]
-        s, n = slot[src[0]], len(src)
-        arr = sum(bits(topo.mask(c, core)) for c in src)
-        m = topo.mask(core, f)
-        g.wait_ge(S.rc, arr)
-        g.remote_dma_fused([put(codes(s, n), [f], m, S.inx)], local_sem=S.sent)
-        g.wait_ge(S.rp, arr)
-        g.remote_dma_fused([put(planes(s, n), [f], m, S.inx)], local_sem=S.sent)
-        g.wait_ge(S.sent, 2 * bits(m))
+        src = indirect.get(mychip, [])
+        mine = [c for c in src if crelay[c] == core]
+        if mine:
+            c = mine[0]
+            m = common(core, far)
+            g.wait_ge(S.rc, E_HOP1)
+            g.remote_dma_fused([put(codes(slot[c]), far_order(core), m, S["in%d" % slot[c]])], local_sem=S.sent)
+            g.wait_ge(S.sent, bits(m))
+        elif src and prelay[mychip] == core:
+            m = common(core, far)
+            g.wait_ge(S.rp, E_HOP1 * len(src))
+            g.remote_dma_fused([put(planes(slot[src[0]], len(src)), far, m, S.inx)], local_sem=S.sent)
+            g.wait_ge(S.sent, bits(m))
         return
 
     v, sc, te, sy = g.vector, g.scalar, g.tensor, g.sync
@@ -197,43 +205,44 @@ def rank_program(g, core, T, topo):
             g.remote_dma_fused([put(part, far, mf, arrive), put(part, mates, mh, arrive)], local_sem=S.sent)
         sent = 2 * (bits(mf) + bits(mh))
     else:
-        via = [relay[f] for f in far]
-        mr = common(core, via)
-        g.remote_dma_fused([put(codes(me), via, mr, S.rc)], local_sem=S.sent)
-        g.remote_dma_fused([put(planes(me), via, mr, S.rp)], local_sem=S.sent)
+        rc, rp = crelay[core], prelay[mychip]
+        mc, mp = some(topo.mask(core, rc), E_HOP1), some(topo.mask(core, rp), E_HOP1, 1)
+        g.remote_dma_fused([put(codes(me), [rc], mc, S.rc)], local_sem=S.sent)
+        g.remote_dma_fused([put(planes(me), [rp], mp, S.rp)], local_sem=S.sent)
         g.remote_dma_fused([put(codes(me), mates, mh, arrive)], local_sem=S.sent)
         g.remote_dma_fused([put(planes(me), mates, mh, arrive)], local_sem=S.sent)
-        sent = 2 * (bits(mr) + bits(mh))
+        sent = bits(mc) + bits(mp) + 2 * bits(mh)
     g.wait_ge(S.sent, sent)
 
     farchip = topo.chip(far[0])
-    order = [(core, None, 0)]
+    order = [(core, [(S.qk, 1), (S.qq, 1)])]
     for c in sorted(mates, key=lambda c: c not in direct[mychip]):
-        order.append((c, S["in%d" % slot[c]], 2 * bits(here_mask(c))))
+        order.append((c, [(S["in%d" % slot[c]], 2 * bits(here_mask(c)))]))
     for c in direct[farchip]:
-        order.append((c, S["in%d" % slot[c]], 2 * bits(common(c, [core] + mates))))
-    for c in indirect[farchip]:
-        order.append((c, S.inx, 2 * bits(topo.mask(relay[core], core))))
-    for i, (c, sem, cnt) in enumerate(order):
+        order.append((c, [(S["in%d" % slot[c]], 2 * bits(common(c, [core] + mates)))]))
+    for c in sorted(indirect[farchip], key=lambda c: far_order(crelay[c]).index(core)):
+        order.append((c, [(S.inx, bits(common(prelay[farchip], [core] + mates))),
+                          (S["in%d" % slot[c]], bits(common(crelay[c], [core] + mates)))]))
+    for i, (c, waits) in enumerate(order):
         j = cores.index(c)
         s = slot[c]
-        banks = [512 * ((4 + 2 * i + h) % 8) for h in range(2)]
-        if i == 0:
-            te.wait_ge(S.qk, 1)
-            te.wait_ge(S.qq, 1)
-        else:
+        y0 = NQ * j
+        for sem, cnt in waits:
             te.wait_ge(sem, cnt)
-        for h in range(2):
+        for h, (a, b) in enumerate(CUTS):
+            bank = 512 * ((4 + 2 * i + h) % 8)
+            acc = T.ps[:, bank:bank + b - a]
             if i >= 4:
                 te.wait_ge(S["e%d_%d" % (i - 4, h)], 1)
-            te.matmul_mx(T.ps[:, banks[h]:banks[h] + H], T.kc[:, 128 * s:128 * s + 128], T.kp[:, 128 * s:128 * s + 128],
-                         T.qc[:, H * h:H * h + H], T.qp[:, H * h:H * h + H], True, True).then_inc(S["p%d_%d" % (i, h)], 1)
-        a = NQ * j
-        v.wait_ge(S["p%d_0" % i], 1)
-        v.tensor_copy(T.ys[:, a:a + H], T.ps[:, banks[0]:banks[0] + H]).then_inc(S["e%d_0" % i], 1)
-        sc.wait_ge(S["p%d_1" % i], 1)
-        sc.activation(T.ys[:, a + H:a + NQ], T.ps[:, banks[1]:banks[1] + H], Copy).then_inc(S["e%d_1" % i], 1)
+            te.matmul_mx(acc, T.kc[:, 128 * s:128 * s + 128], T.kp[:, 128 * s:128 * s + 128],
+                         T.qc[:, a:b], T.qp[:, a:b], True, True).then_inc(S["p%d_%d" % (i, h)], 1)
+            if h == 0:
+                v.wait_ge(S["p%d_0" % i], 1)
+                v.tensor_copy(T.ys[:, y0 + a:y0 + b], acc).then_inc(S["e%d_0" % i], 1)
+            else:
+                sc.wait_ge(S["p%d_1" % i], 1)
+                sc.activation(T.ys[:, y0 + a:y0 + b], acc, Copy).then_inc(S["e%d_1" % i], 1)
         sy.wait_ge(S["e%d_0" % i], 1)
         sy.wait_ge(S["e%d_1" % i], 1)
-        sy.dma_start(T.y[:, a:a + NQ], T.ys[:, a:a + NQ]).then_inc(S.st, 16)
+        sy.dma_start(T.y[:, y0:y0 + NQ], T.ys[:, y0:y0 + NQ]).then_inc(S.st, 16)
     sy.wait_ge(S.st, 16 * N)

@@ -31,9 +31,10 @@ SCRATCH = {
     "ps": ("psum", [128, 4096], "float32"),
 }
 SEMAPHORES = (
-    ["l_xk", "l_wa", "l_wb", "l_cs", "l_sn", "l_xq", "zero", "da", "db0", "db1", "sa", "sb0", "sb1", "tk", "qk", "qq",
-     "qx", "rc", "rp", "inx", "sent", "st"]
-    + ["qw%d" % i for i in range(4)] + ["z%d" % i for i in range(4)] + ["in%d" % i for i in range(N)]
+    ["l_xk", "l_cs", "l_sn", "l_xq", "zero", "da0", "da1", "db0", "db1", "sa0", "sa1", "sb0", "sb1", "sb2",
+     "tk", "qk", "qq", "qx", "rc", "rp", "inx", "sent", "st"]
+    + ["l_w%d" % i for i in range(4)] + ["qw%d" % i for i in range(4)] + ["z%d" % i for i in range(4)]
+    + ["in%d" % i for i in range(N)]
     + ["p%d_%d" % (i, h) for i in range(N) for h in range(2)] + ["e%d_%d" % (i, h) for i in range(N) for h in range(2)])
 
 
@@ -95,12 +96,13 @@ def rank_program(g, core, T, topo):
             m &= topo.mask(src, d)
         return m
 
-    def here_mask(src):
+    def here_masks(src):
         ms = [c for c in cores if topo.chip(c) == topo.chip(src) and c != src]
         m = common(src, ms)
         if src in direct[topo.chip(src)]:
             m &= ~common(src, [c for c in cores if topo.chip(c) != topo.chip(src)])
-        return m
+            return m, m
+        return m, some(m, E_HOP1)
 
     def far_order(relay):
         fs = [c for c in cores if topo.chip(c) != topo.chip(relay)]
@@ -129,11 +131,16 @@ def rank_program(g, core, T, topo):
     K = 0.019
     me = slot[core]
 
+    def load_w(q, i):
+        q.dma_start(T.wks[:, 512 * i:512 * i + 512], T.wk[:, 512 * i:512 * i + 512]).then_inc(S["l_w%d" % i], 16)
+
     sy.dma_start(T.xks[:], T.xk[:]).then_inc(S.l_xk, 16)
-    sc.dma_start(T.wks[:, 0:1024], T.wk[:, 0:1024]).then_inc(S.l_wa, 16)
-    sy.dma_start(T.css[:], T.cs[:]).then_inc(S.l_cs, 16)
-    sc.dma_start(T.sns[:], T.sn[:]).then_inc(S.l_sn, 16)
-    sy.dma_start(T.wks[:, 1024:2048], T.wk[:, 1024:2048]).then_inc(S.l_wb, 16)
+    load_w(sc, 0)
+    load_w(sy, 1)
+    sc.dma_start(T.css[:], T.cs[:]).then_inc(S.l_cs, 16)
+    sy.dma_start(T.sns[:], T.sn[:]).then_inc(S.l_sn, 16)
+    load_w(sc, 2)
+    load_w(sy, 3)
     sy.dma_start(T.xqs[:], T.xq[:]).then_inc(S.l_xq, 16)
 
     def zb(i):
@@ -141,6 +148,7 @@ def rank_program(g, core, T, topo):
 
     def qw(i):
         a = 128 * i
+        v.wait_ge(S["l_w%d" % i], 16)
         v.quantize_mx(T.wc[:, a:a + 128], T.wp[:, a:a + 128], T.wks[:, 4 * a:4 * a + 512]).then_inc(S["qw%d" % i], 1)
 
     te.wait_ge(S.qx, 1)
@@ -149,75 +157,81 @@ def rank_program(g, core, T, topo):
         te.wait_ge(S["qw%d" % i], 1)
         te.matmul_mx(zb(i), T.wc[:, a:a + 128], T.wp[:, a:a + 128], T.xc[:], T.xp[:], True, True).then_inc(S["z%d" % i], 1)
 
+    def scan(out, data, a, b, done):
+        v.tensor_tensor_scan(out[:, a:b], T.rot[:, a:b], data[:, a:b], 0.0, mult, add).then_inc(done, 1)
+
     v.memset(T.rot[:], 0.0).then_inc(S.zero, 1)
     v.wait_ge(S.l_xk, 16)
     v.quantize_mx(T.xc[:], T.xp[:], T.xks[:]).then_inc(S.qx, 1)
-    v.wait_ge(S.l_wa, 16)
     qw(0)
     qw(1)
+    v.wait_ge(S.zero, 1)
     v.wait_ge(S.l_cs, 16)
+    v.tensor_copy(T.rot[:, 257:512:2], T.css[:]).then_inc(S.da1, 1)
     v.wait_ge(S.l_sn, 16)
+    v.tensor_scalar(T.rot[:, 1:256:2], T.sns[:], -1.0, None, mult).then_inc(S.da0, 1)
     v.wait_ge(S.z0, 1)
-    v.tensor_tensor(T.da[:, 1:256:2], zb(0), T.css[:], mult).then_inc(S.da, 1)
-    v.tensor_tensor(T.da[:, 257:512:2], zb(0), T.sns[:], mult).then_inc(S.da, 1)
-    v.wait_ge(S.da, 6)
-    v.tensor_tensor_scan(T.ra[:], T.rot[:], T.da[:], 0.0, mult, add).then_inc(S.sa, 1)
-    v.wait_ge(S.l_wb, 16)
+    v.tensor_tensor(T.da[:, 1:256:2], zb(0), T.css[:], mult).then_inc(S.da0, 1)
+    v.tensor_tensor(T.da[:, 257:512:2], zb(0), T.sns[:], mult).then_inc(S.da1, 1)
     qw(2)
+    v.wait_ge(S.da0, 3)
+    scan(T.ra, T.da, 0, 256, S.sa0)
     qw(3)
+    v.wait_ge(S.da1, 3)
+    scan(T.ra, T.da, 256, 512, S.sa1)
     v.wait_ge(S.z2, 1)
     v.tensor_tensor(T.db[:, 1:256:2], zb(2), T.css[:], mult).then_inc(S.db0, 1)
     v.tensor_tensor(T.db[:, 257:512:2], zb(2), T.sns[:], mult).then_inc(S.db1, 1)
     v.wait_ge(S.db0, 2)
-    v.tensor_tensor_scan(T.rb[:, 0:256], T.rot[:, 0:256], T.db[:, 0:256], 0.0, mult, add).then_inc(S.sb0, 1)
+    scan(T.rb, T.db, 0, 256, S.sb0)
     v.wait_ge(S.db1, 2)
-    v.tensor_tensor_scan(T.rb[:, 256:512], T.rot[:, 256:512], T.db[:, 256:512], 0.0, mult, add).then_inc(S.sb1, 1)
-    v.wait_ge(S.sb1, 1)
-    v.tensor_scalar(T.kt[:, 3:512:4], T.rb[:, 257:512:2], K, None, mult).then_inc(S.tk, 1)
-    v.wait_ge(S.tk, 4)
+    scan(T.rb, T.db, 256, 384, S.sb1)
+    scan(T.rb, T.db, 384, 512, S.sb2)
+    v.wait_ge(S.sb2, 1)
+    v.tensor_scalar(T.kt[:, 259:512:4], T.rb[:, 385:512:2], K, None, mult).then_inc(S.tk, 1)
+    v.wait_ge(S.tk, 5)
     v.quantize_mx(T.kc[:, 128 * me:128 * me + 128], T.kp[:, 128 * me:128 * me + 128], T.kt[:]).then_inc(S.qk, 1)
     v.wait_ge(S.l_xq, 16)
     v.quantize_mx(T.qc[:], T.qp[:], T.xqs[:]).then_inc(S.qq, 1)
 
-    sc.wait_ge(S.zero, 1)
-    sc.wait_ge(S.l_cs, 16)
-    sc.activation(T.rot[:, 257:512:2], T.css[:], Copy).then_inc(S.da, 1)
-    sc.wait_ge(S.l_sn, 16)
-    sc.activation(T.rot[:, 1:256:2], T.sns[:], Copy, scale=-1.0).then_inc(S.da, 1)
     sc.wait_ge(S.z1, 1)
-    sc.activation(T.da[:, 0:256:2], zb(1), Copy).then_inc(S.da, 1)
-    sc.activation(T.da[:, 256:512:2], zb(1), Copy).then_inc(S.da, 1)
-    sc.wait_ge(S.sa, 1)
+    sc.activation(T.da[:, 0:256:2], zb(1), Copy).then_inc(S.da0, 1)
+    sc.activation(T.da[:, 256:512:2], zb(1), Copy).then_inc(S.da1, 1)
+    sc.wait_ge(S.sa0, 1)
     sc.activation(T.kt[:, 0:512:4], T.ra[:, 1:256:2], Copy, scale=K).then_inc(S.tk, 1)
-    sc.activation(T.kt[:, 1:512:4], T.ra[:, 257:512:2], Copy, scale=K).then_inc(S.tk, 1)
     sc.wait_ge(S.z3, 1)
     sc.activation(T.db[:, 0:256:2], zb(3), Copy).then_inc(S.db0, 1)
     sc.activation(T.db[:, 256:512:2], zb(3), Copy).then_inc(S.db1, 1)
+    sc.wait_ge(S.sa1, 1)
+    sc.activation(T.kt[:, 1:512:4], T.ra[:, 257:512:2], Copy, scale=K).then_inc(S.tk, 1)
     sc.wait_ge(S.sb0, 1)
     sc.activation(T.kt[:, 2:512:4], T.rb[:, 1:256:2], Copy, scale=K).then_inc(S.tk, 1)
+    sc.wait_ge(S.sb1, 1)
+    sc.activation(T.kt[:, 3:256:4], T.rb[:, 257:384:2], Copy, scale=K).then_inc(S.tk, 1)
 
     g.wait_ge(S.qk, 1)
     arrive = S["in%d" % me]
-    mh = here_mask(core)
+    mh, mhp = here_masks(core)
     if core in direct[mychip]:
         mf = common(core, far)
-        for part in (codes(me), planes(me)):
-            g.remote_dma_fused([put(part, far, mf, arrive), put(part, mates, mh, arrive)], local_sem=S.sent)
-        sent = 2 * (bits(mf) + bits(mh))
+        g.remote_dma_fused([put(codes(me), far, mf, arrive)], local_sem=S.sent)
+        g.remote_dma_fused([put(planes(me), far, mf, arrive)], local_sem=S.sent)
+        g.remote_dma_fused([put(codes(me), mates, mh, arrive)], local_sem=S.sent)
+        g.remote_dma_fused([put(planes(me), mates, mhp, arrive)], local_sem=S.sent)
+        sent = 2 * bits(mf) + bits(mh) + bits(mhp)
     else:
         rc, rp = crelay[core], prelay[mychip]
         mc, mp = some(topo.mask(core, rc), E_HOP1), some(topo.mask(core, rp), E_HOP1, 1)
         g.remote_dma_fused([put(codes(me), [rc], mc, S.rc)], local_sem=S.sent)
-        g.remote_dma_fused([put(planes(me), [rp], mp, S.rp)], local_sem=S.sent)
+        g.remote_dma_fused([put(planes(me), [rp], mp, S.rp), put(planes(me), mates, mhp, arrive)], local_sem=S.sent)
         g.remote_dma_fused([put(codes(me), mates, mh, arrive)], local_sem=S.sent)
-        g.remote_dma_fused([put(planes(me), mates, mh, arrive)], local_sem=S.sent)
-        sent = bits(mc) + bits(mp) + 2 * bits(mh)
+        sent = bits(mc) + bits(mp) + bits(mhp) + bits(mh)
     g.wait_ge(S.sent, sent)
 
     farchip = topo.chip(far[0])
     order = [(core, [(S.qk, 1), (S.qq, 1)])]
-    for c in sorted(mates, key=lambda c: c not in direct[mychip]):
-        order.append((c, [(S["in%d" % slot[c]], 2 * bits(here_mask(c)))]))
+    for c in sorted(mates, key=lambda c: c in direct[mychip]):
+        order.append((c, [(S["in%d" % slot[c]], sum(bits(m) for m in here_masks(c)))]))
     for c in direct[farchip]:
         order.append((c, [(S["in%d" % slot[c]], 2 * bits(common(c, [core] + mates)))]))
     for c in sorted(indirect[farchip], key=lambda c: far_order(crelay[c]).index(core)):

@@ -5,7 +5,6 @@ N = 6
 NQ = 384
 CUTS = ((0, 256), (256, 384))
 SIM_CORES = 16
-E_HOP1 = 8
 
 SCRATCH = {
     "xks": ("sbuf", [128, 512], "bfloat16"),
@@ -21,7 +20,8 @@ SCRATCH = {
     "qp": ("sbuf", [128, NQ], "uint8"),
     "kc": ("sbuf", [128, N * 128], "float8_e4m3fn_x4"),
     "kp": ("sbuf", [128, N * 128], "uint8"),
-    "rot": ("sbuf", [128, 512], "bfloat16"),
+    "za": ("sbuf", [128, 256], "float32"),
+    "zb": ("sbuf", [128, 256], "float32"),
     "da": ("sbuf", [128, 512], "float32"),
     "db": ("sbuf", [128, 512], "float32"),
     "ra": ("sbuf", [128, 512], "float32"),
@@ -31,10 +31,10 @@ SCRATCH = {
     "ps": ("psum", [128, 4096], "float32"),
 }
 SEMAPHORES = (
-    ["l_xk", "l_cs", "l_sn", "l_xq", "zero", "da0", "da1", "db0", "db1", "sa0", "sa1", "sb0", "sb1", "sb2",
-     "tk", "qk", "qq", "qx", "rc", "rp", "inx", "sent", "st"]
-    + ["l_w%d" % i for i in range(4)] + ["qw%d" % i for i in range(4)] + ["z%d" % i for i in range(4)]
-    + ["in%d" % i for i in range(N)]
+    ["l_xk", "l_cs", "l_sn", "l_xq", "l_w01", "l_w2", "l_w3", "zero", "zc1", "zc3", "da0", "da1", "db0", "db1",
+     "sa0", "sa1", "sb0", "sb1", "sb2", "tk", "qk", "qq", "qx", "sent", "st"]
+    + ["qw%d" % i for i in range(4)] + ["z%d" % i for i in range(4)]
+    + ["%s%d" % (k, i) for k in "cp" for i in range(N)]
     + ["p%d_%d" % (i, h) for i in range(N) for h in range(2)] + ["e%d_%d" % (i, h) for i in range(N) for h in range(2)])
 
 
@@ -42,87 +42,78 @@ def bits(mask):
     return bin(mask).count("1")
 
 
-def some(mask, n, part=0):
-    e = [i for i in range(mask.bit_length()) if mask >> i & 1]
-    k = part * n % len(e)
-    return sum(1 << i for i in e[k:k + n])
-
-
-def plan(T, topo):
+def roles(T, topo):
     cores = list(T.cores)
     chips = sorted(set(topo.chip(c) for c in cores))
-    direct, indirect, crelay, prelay = {}, {}, {}, {}
+    R, slot = {}, {}
     for ch in chips:
         here = [c for c in cores if topo.chip(c) == ch]
         far = [c for c in cores if topo.chip(c) != ch]
-        direct[ch] = [c for c in here if all(topo.may_write(c, f) for f in far)]
-        indirect[ch] = [c for c in here if c not in direct[ch]]
+        d = [c for c in here if all(topo.may_write(c, f) for f in far)][0]
+        ind = sorted([c for c in here if c != d], key=lambda c: topo.die(c) != topo.die(d))
         free = [c for c in range(SIM_CORES) if topo.chip(c) == ch and c not in cores
                 and all(topo.may_write(c, f) for f in far)]
-        for c in indirect[ch]:
-            crelay[c] = sorted(free, key=lambda r: (topo.die(r) != topo.die(c), r))[0]
-            free.remove(crelay[c])
-        prelay[ch] = free[0]
-    order = [c for ch in chips for c in indirect[ch]] + [c for ch in chips for c in direct[ch]]
-    slot = {c: i for i, c in enumerate(order)}
-    return direct, indirect, crelay, prelay, slot
+        rel = []
+        for c in ind:
+            rel.append(sorted(free, key=lambda r: (topo.die(r) != topo.die(c), r))[0])
+            free.remove(rel[-1])
+        R[ch] = {"d": d, "i1": ind[0], "i2": ind[1], "r1": rel[0], "r2": rel[1], "x": free[0]}
+        for c in (ind[0], ind[1], d):
+            slot[c] = len(slot)
+    return R, slot
+
+
+def routes(topo, R, slot):
+    calls = {}
+    for ch in R:
+        h, f = R[ch], R[[k for k in R if k != ch][0]]
+        d, i1, i2, x = h["d"], h["i1"], h["i2"], h["x"]
+        A, B, D, F = slot[i1], slot[i2], slot[d], slot[f["d"]]
+        out = topo.mask(d, f["d"])
+        stay = topo.mask(d, i1) & ~out
+        calls[d] = [("c", D, 1, [f["d"]], out), ("p", D, 1, [f["d"]], out),
+                    ("c", D, 1, [i1, i2], stay), ("p", D, 1, [i1, i2], stay),
+                    ("c", F, 1, [i1, i2], out), ("p", F, 1, [i1, i2], stay),
+                    ("c", B, 1, [f["d"]], out)]
+        calls[i1] = [("c", A, 1, [h["r1"]], out), ("p", A, 1, [x, d, i2], stay), ("c", A, 1, [d, i2], out | stay),
+                     ("c", A, 1, [x], stay)]
+        calls[i2] = [("c", B, 1, [h["r2"]], out), ("p", B, 1, [x, d, i1], stay), ("c", B, 1, [d, i1], out | stay)]
+        calls[h["r1"]] = [("c", A, 1, [f["i1"], f["d"]], out)]
+        calls[h["r2"]] = [("c", B, 1, [f["i2"], f["i1"]], out)]
+        calls[x] = [("p", A, 2, [f["i1"], f["i2"], f["d"]], out), ("c", A, 1, [f["i2"]], out)]
+    return calls
 
 
 def rank_program(g, core, T, topo):
     S = T.sem
     rank = T.rank_of(core)
-    cores = list(T.cores)
     mychip = topo.chip(core)
-    direct, indirect, crelay, prelay, slot = plan(T, topo)
-    mates = [c for c in cores if topo.chip(c) == mychip and c != core]
-    far = [c for c in cores if topo.chip(c) != mychip]
+    R, slot = roles(T, topo)
+    calls = routes(topo, R, slot)
+    lands = {}
+    for cl in calls.values():
+        for k, s, n, dsts, m in cl:
+            if core in dsts:
+                for i in range(n):
+                    lands[k, s + i] = (S["%s%d" % (k, s)], bits(m))
 
-    def codes(s):
-        return T.kc[:, 128 * s:128 * (s + 1)].bitcast(dt.uint8)
-
-    def planes(s, n=1):
-        return T.kp[:, 128 * s:128 * (s + n)]
-
-    def put(view, dsts, mask, sem):
-        ids = []
-        for d in dsts:
-            rid, pid, _ = topo.addr(d)
-            ids.append(DstId(rid=rid, pnc=pid))
-        return RemoteDMATransfer(dst_ids=ids, dma_engine_mask=mask, remote_sem=sem, srcs=[view], dsts=[view] * len(ids))
-
-    def common(src, dsts):
-        m = topo.mask(src, dsts[0])
-        for d in dsts[1:]:
-            m &= topo.mask(src, d)
-        return m
-
-    def here_masks(src):
-        ms = [c for c in cores if topo.chip(c) == topo.chip(src) and c != src]
-        m = common(src, ms)
-        if src in direct[topo.chip(src)]:
-            m &= ~common(src, [c for c in cores if topo.chip(c) != topo.chip(src)])
-            return m, m
-        return m, some(m, E_HOP1)
-
-    def far_order(relay):
-        fs = [c for c in cores if topo.chip(c) != topo.chip(relay)]
-        fs = sorted(fs, key=lambda f: -topo.die(f))
-        return fs if topo.die(relay) == topo.die(fs[0]) else fs[::-1]
+    def send():
+        for k, s, n, dsts, m in calls[core]:
+            if rank is None or s != slot[core]:
+                for sem, cnt in [lands[k, s + i] for i in range(n)]:
+                    g.wait_ge(sem, cnt)
+            view = T.kc[:, 128 * s:128 * (s + n)].bitcast(dt.uint8) if k == "c" else T.kp[:, 128 * s:128 * (s + n)]
+            ids = []
+            for c in dsts:
+                rid, pid, _ = topo.addr(c)
+                ids.append(DstId(rid=rid, pnc=pid))
+            g.remote_dma_fused([RemoteDMATransfer(dst_ids=ids, dma_engine_mask=m, remote_sem=S["%s%d" % (k, s)],
+                                                  srcs=[view], dsts=[view] * len(ids))], local_sem=S.sent)
+        g.wait_ge(S.sent, sum(bits(c[4]) for c in calls[core]))
 
     if rank is None:
-        src = indirect.get(mychip, [])
-        mine = [c for c in src if crelay[c] == core]
-        if mine:
-            c = mine[0]
-            m = common(core, far)
-            g.wait_ge(S.rc, E_HOP1)
-            g.remote_dma_fused([put(codes(slot[c]), far_order(core), m, S["in%d" % slot[c]])], local_sem=S.sent)
-            g.wait_ge(S.sent, bits(m))
-        elif src and prelay[mychip] == core:
-            m = common(core, far)
-            g.wait_ge(S.rp, E_HOP1 * len(src))
-            g.remote_dma_fused([put(planes(slot[src[0]], len(src)), far, m, S.inx)], local_sem=S.sent)
-            g.wait_ge(S.sent, bits(m))
+        if core in calls:
+            send()
         return
 
     v, sc, te, sy = g.vector, g.scalar, g.tensor, g.sync
@@ -131,16 +122,12 @@ def rank_program(g, core, T, topo):
     K = 0.019
     me = slot[core]
 
-    def load_w(q, i):
-        q.dma_start(T.wks[:, 512 * i:512 * i + 512], T.wk[:, 512 * i:512 * i + 512]).then_inc(S["l_w%d" % i], 16)
-
     sy.dma_start(T.xks[:], T.xk[:]).then_inc(S.l_xk, 16)
-    load_w(sc, 0)
-    load_w(sy, 1)
-    sc.dma_start(T.css[:], T.cs[:]).then_inc(S.l_cs, 16)
+    sc.dma_start(T.wks[:, 0:1024], T.wk[:, 0:1024]).then_inc(S.l_w01, 16)
     sy.dma_start(T.sns[:], T.sn[:]).then_inc(S.l_sn, 16)
-    load_w(sc, 2)
-    load_w(sy, 3)
+    sy.dma_start(T.css[:], T.cs[:]).then_inc(S.l_cs, 16)
+    sc.dma_start(T.wks[:, 1024:1536], T.wk[:, 1024:1536]).then_inc(S.l_w2, 16)
+    sy.dma_start(T.wks[:, 1536:2048], T.wk[:, 1536:2048]).then_inc(S.l_w3, 16)
     sy.dma_start(T.xqs[:], T.xq[:]).then_inc(S.l_xq, 16)
 
     def zb(i):
@@ -148,7 +135,7 @@ def rank_program(g, core, T, topo):
 
     def qw(i):
         a = 128 * i
-        v.wait_ge(S["l_w%d" % i], 16)
+        v.wait_ge((S.l_w01, S.l_w01, S.l_w2, S.l_w3)[i], 16)
         v.quantize_mx(T.wc[:, a:a + 128], T.wp[:, a:a + 128], T.wks[:, 4 * a:4 * a + 512]).then_inc(S["qw%d" % i], 1)
 
     te.wait_ge(S.qx, 1)
@@ -157,36 +144,36 @@ def rank_program(g, core, T, topo):
         te.wait_ge(S["qw%d" % i], 1)
         te.matmul_mx(zb(i), T.wc[:, a:a + 128], T.wp[:, a:a + 128], T.xc[:], T.xp[:], True, True).then_inc(S["z%d" % i], 1)
 
-    def scan(out, data, a, b, done):
-        v.tensor_tensor_scan(out[:, a:b], T.rot[:, a:b], data[:, a:b], 0.0, mult, add).then_inc(done, 1)
+    def scan(out, z, z0, data, a, b, done):
+        v.tensor_tensor_scan(out[:, a:b], z[:, a - z0:b - z0], data[:, a:b], 0.0, mult, add).then_inc(done, 1)
 
-    v.memset(T.rot[:], 0.0).then_inc(S.zero, 1)
+    v.memset(T.za[:], 0.0).then_inc(S.zero, 1)
+    v.memset(T.zb[:], 0.0).then_inc(S.zero, 1)
     v.wait_ge(S.l_xk, 16)
     v.quantize_mx(T.xc[:], T.xp[:], T.xks[:]).then_inc(S.qx, 1)
     qw(0)
     qw(1)
-    v.wait_ge(S.zero, 1)
-    v.wait_ge(S.l_cs, 16)
-    v.tensor_copy(T.rot[:, 257:512:2], T.css[:]).then_inc(S.da1, 1)
-    v.wait_ge(S.l_sn, 16)
-    v.tensor_scalar(T.rot[:, 1:256:2], T.sns[:], -1.0, None, mult).then_inc(S.da0, 1)
-    v.wait_ge(S.z0, 1)
-    v.tensor_tensor(T.da[:, 1:256:2], zb(0), T.css[:], mult).then_inc(S.da0, 1)
-    v.tensor_tensor(T.da[:, 257:512:2], zb(0), T.sns[:], mult).then_inc(S.da1, 1)
     qw(2)
-    v.wait_ge(S.da0, 3)
-    scan(T.ra, T.da, 0, 256, S.sa0)
+    v.wait_ge(S.z0, 1)
+    v.wait_ge(S.l_sn, 16)
+    v.tensor_tensor(T.da[:, 257:512:2], zb(0), T.sns[:], mult).then_inc(S.da1, 1)
+    v.wait_ge(S.l_cs, 16)
+    v.tensor_tensor(T.da[:, 1:256:2], zb(0), T.css[:], mult).then_inc(S.da0, 1)
     qw(3)
-    v.wait_ge(S.da1, 3)
-    scan(T.ra, T.da, 256, 512, S.sa1)
     v.wait_ge(S.z2, 1)
     v.tensor_tensor(T.db[:, 1:256:2], zb(2), T.css[:], mult).then_inc(S.db0, 1)
     v.tensor_tensor(T.db[:, 257:512:2], zb(2), T.sns[:], mult).then_inc(S.db1, 1)
+    v.wait_ge(S.zc1, 1)
+    v.wait_ge(S.da0, 2)
+    scan(T.ra, T.za, 0, T.da, 0, 256, S.sa0)
+    v.wait_ge(S.da1, 2)
+    scan(T.ra, T.za, 256, T.da, 256, 512, S.sa1)
+    v.wait_ge(S.zc3, 1)
     v.wait_ge(S.db0, 2)
-    scan(T.rb, T.db, 0, 256, S.sb0)
+    scan(T.rb, T.zb, 0, T.db, 0, 256, S.sb0)
     v.wait_ge(S.db1, 2)
-    scan(T.rb, T.db, 256, 384, S.sb1)
-    scan(T.rb, T.db, 384, 512, S.sb2)
+    scan(T.rb, T.zb, 256, T.db, 256, 384, S.sb1)
+    scan(T.rb, T.zb, 256, T.db, 384, 512, S.sb2)
     v.wait_ge(S.sb2, 1)
     v.tensor_scalar(T.kt[:, 259:512:4], T.rb[:, 385:512:2], K, None, mult).then_inc(S.tk, 1)
     v.wait_ge(S.tk, 5)
@@ -194,63 +181,43 @@ def rank_program(g, core, T, topo):
     v.wait_ge(S.l_xq, 16)
     v.quantize_mx(T.qc[:], T.qp[:], T.xqs[:]).then_inc(S.qq, 1)
 
+    sc.wait_ge(S.l_sn, 16)
+    sc.activation(T.da[:, 0:256:2], T.sns[:], Copy, scale=-1.0).then_inc(S.da0, 1)
+    sc.activation(T.db[:, 0:256:2], T.sns[:], Copy, scale=-1.0).then_inc(S.db0, 1)
+    sc.wait_ge(S.zero, 2)
     sc.wait_ge(S.z1, 1)
-    sc.activation(T.da[:, 0:256:2], zb(1), Copy).then_inc(S.da0, 1)
-    sc.activation(T.da[:, 256:512:2], zb(1), Copy).then_inc(S.da1, 1)
-    sc.wait_ge(S.sa0, 1)
-    sc.activation(T.kt[:, 0:512:4], T.ra[:, 1:256:2], Copy, scale=K).then_inc(S.tk, 1)
+    sc.activation(T.za[:, 1:256:2], zb(1), Copy).then_inc(S.zc1, 1)
+    sc.wait_ge(S.l_cs, 16)
+    sc.activation(T.db[:, 256:512:2], T.css[:], Copy).then_inc(S.db1, 1)
+    sc.activation(T.da[:, 256:512:2], T.css[:], Copy).then_inc(S.da1, 1)
     sc.wait_ge(S.z3, 1)
-    sc.activation(T.db[:, 0:256:2], zb(3), Copy).then_inc(S.db0, 1)
-    sc.activation(T.db[:, 256:512:2], zb(3), Copy).then_inc(S.db1, 1)
-    sc.wait_ge(S.sa1, 1)
-    sc.activation(T.kt[:, 1:512:4], T.ra[:, 257:512:2], Copy, scale=K).then_inc(S.tk, 1)
-    sc.wait_ge(S.sb0, 1)
-    sc.activation(T.kt[:, 2:512:4], T.rb[:, 1:256:2], Copy, scale=K).then_inc(S.tk, 1)
+    sc.activation(T.zb[:, 1:256:2], zb(3), Copy).then_inc(S.zc3, 1)
+    for b, (done, r) in enumerate(((S.sa0, T.ra[:, 1:256:2]), (S.sa1, T.ra[:, 257:512:2]), (S.sb0, T.rb[:, 1:256:2]))):
+        sc.wait_ge(done, 1)
+        sc.activation(T.kt[:, b:512:4], r, Copy, scale=K).then_inc(S.tk, 1)
     sc.wait_ge(S.sb1, 1)
     sc.activation(T.kt[:, 3:256:4], T.rb[:, 257:384:2], Copy, scale=K).then_inc(S.tk, 1)
 
     g.wait_ge(S.qk, 1)
-    arrive = S["in%d" % me]
-    mh, mhp = here_masks(core)
-    if core in direct[mychip]:
-        mf = common(core, far)
-        g.remote_dma_fused([put(codes(me), far, mf, arrive)], local_sem=S.sent)
-        g.remote_dma_fused([put(planes(me), far, mf, arrive)], local_sem=S.sent)
-        g.remote_dma_fused([put(codes(me), mates, mh, arrive)], local_sem=S.sent)
-        g.remote_dma_fused([put(planes(me), mates, mhp, arrive)], local_sem=S.sent)
-        sent = 2 * bits(mf) + bits(mh) + bits(mhp)
-    else:
-        rc, rp = crelay[core], prelay[mychip]
-        mc, mp = some(topo.mask(core, rc), E_HOP1), some(topo.mask(core, rp), E_HOP1, 1)
-        g.remote_dma_fused([put(codes(me), [rc], mc, S.rc)], local_sem=S.sent)
-        g.remote_dma_fused([put(planes(me), [rp], mp, S.rp), put(planes(me), mates, mhp, arrive)], local_sem=S.sent)
-        g.remote_dma_fused([put(codes(me), mates, mh, arrive)], local_sem=S.sent)
-        sent = bits(mc) + bits(mp) + bits(mhp) + bits(mh)
-    g.wait_ge(S.sent, sent)
+    send()
 
-    farchip = topo.chip(far[0])
-    order = [(core, [(S.qk, 1), (S.qq, 1)])]
-    for c in sorted(mates, key=lambda c: c in direct[mychip]):
-        order.append((c, [(S["in%d" % slot[c]], sum(bits(m) for m in here_masks(c)))]))
-    for c in direct[farchip]:
-        order.append((c, [(S["in%d" % slot[c]], 2 * bits(common(c, [core] + mates)))]))
-    for c in sorted(indirect[farchip], key=lambda c: far_order(crelay[c]).index(core)):
-        order.append((c, [(S.inx, bits(common(prelay[farchip], [core] + mates))),
-                          (S["in%d" % slot[c]], bits(common(crelay[c], [core] + mates)))]))
-    for i, (c, waits) in enumerate(order):
-        j = cores.index(c)
+    h, f = R[mychip], R[[k for k in R if k != mychip][0]]
+    order = [core] + {h["d"]: [h["i1"], f["d"], h["i2"], f["i1"], f["i2"]],
+                      h["i1"]: [h["i2"], h["d"], f["d"], f["i1"], f["i2"]],
+                      h["i2"]: [h["i1"], h["d"], f["d"], f["i2"], f["i1"]]}[core]
+    for i, c in enumerate(order):
+        y0 = NQ * list(T.cores).index(c)
         s = slot[c]
-        y0 = NQ * j
-        for sem, cnt in waits:
+        for sem, cnt in ([(S.qk, 1), (S.qq, 1)] if c == core else [lands["p", s], lands["c", s]]):
             te.wait_ge(sem, cnt)
-        for h, (a, b) in enumerate(CUTS):
-            bank = 512 * ((4 + 2 * i + h) % 8)
+        for n, (a, b) in enumerate(CUTS):
+            bank = 512 * ((4 + 2 * i + n) % 8)
             acc = T.ps[:, bank:bank + b - a]
             if i >= 4:
-                te.wait_ge(S["e%d_%d" % (i - 4, h)], 1)
+                te.wait_ge(S["e%d_%d" % (i - 4, n)], 1)
             te.matmul_mx(acc, T.kc[:, 128 * s:128 * s + 128], T.kp[:, 128 * s:128 * s + 128],
-                         T.qc[:, a:b], T.qp[:, a:b], True, True).then_inc(S["p%d_%d" % (i, h)], 1)
-            if h == 0:
+                         T.qc[:, a:b], T.qp[:, a:b], True, True).then_inc(S["p%d_%d" % (i, n)], 1)
+            if n == 0:
                 v.wait_ge(S["p%d_0" % i], 1)
                 v.tensor_copy(T.ys[:, y0 + a:y0 + b], acc).then_inc(S["e%d_0" % i], 1)
             else:

from concourse.bass import DstId, RemoteDMATransfer
from concourse.mybir import dt, AluOpType, ActivationFunctionType

N = 6
NQ = 384
CUTS = ((0, 256), (256, 384))
SIM_CORES = 16

SCRATCH = {
    "xks": ("sbuf", [128, 512], "bfloat16"),
    "wks": ("sbuf", [128, 2048], "bfloat16"),
    "xqs": ("sbuf", [128, 4 * NQ], "bfloat16"),
    "css": ("sbuf", [128, 128], "bfloat16"),
    "sns": ("sbuf", [128, 128], "bfloat16"),
    "xc": ("sbuf", [128, 128], "float8_e4m3fn_x4"),
    "xp": ("sbuf", [128, 128], "uint8"),
    "wc": ("sbuf", [128, 512], "float8_e4m3fn_x4"),
    "wp": ("sbuf", [128, 512], "uint8"),
    "qc": ("sbuf", [128, NQ], "float8_e4m3fn_x4"),
    "qp": ("sbuf", [128, NQ], "uint8"),
    "kc": ("sbuf", [128, N * 128], "float8_e4m3fn_x4"),
    "kp": ("sbuf", [128, N * 128], "uint8"),
    "za": ("sbuf", [128, 256], "float32"),
    "zb": ("sbuf", [128, 256], "float32"),
    "da": ("sbuf", [128, 512], "float32"),
    "db": ("sbuf", [128, 512], "float32"),
    "ra": ("sbuf", [128, 512], "float32"),
    "rb": ("sbuf", [128, 512], "float32"),
    "kt": ("sbuf", [128, 512], "bfloat16"),
    "ys": ("sbuf", [128, N * NQ], "float32"),
    "ps": ("psum", [128, 4096], "float32"),
}
SEMAPHORES = (
    ["l_xk", "l_cs", "l_sn", "l_xq", "l_w01", "l_w2", "l_w3", "zero", "zc1", "zc3", "da0", "da1", "db0", "db1",
     "sa0", "sa1", "sb0", "sb1", "sb2", "tk", "qk", "qq", "qx", "sent", "st"]
    + ["qw%d" % i for i in range(4)] + ["z%d" % i for i in range(4)]
    + ["%s%d" % (k, i) for k in "cp" for i in range(N)]
    + ["p%d_%d" % (i, h) for i in range(N) for h in range(2)] + ["e%d_%d" % (i, h) for i in range(N) for h in range(2)])


def bits(mask):
    return bin(mask).count("1")


def roles(T, topo):
    cores = list(T.cores)
    chips = sorted(set(topo.chip(c) for c in cores))
    R, slot = {}, {}
    for ch in chips:
        here = [c for c in cores if topo.chip(c) == ch]
        far = [c for c in cores if topo.chip(c) != ch]
        d = [c for c in here if all(topo.may_write(c, f) for f in far)][0]
        ind = sorted([c for c in here if c != d], key=lambda c: topo.die(c) != topo.die(d))
        free = [c for c in range(SIM_CORES) if topo.chip(c) == ch and c not in cores
                and all(topo.may_write(c, f) for f in far)]
        rel = []
        for c in ind:
            rel.append(sorted(free, key=lambda r: (topo.die(r) != topo.die(c), r))[0])
            free.remove(rel[-1])
        R[ch] = {"d": d, "i1": ind[0], "i2": ind[1], "r1": rel[0], "r2": rel[1], "x": free[0]}
        for c in (ind[0], ind[1], d):
            slot[c] = len(slot)
    return R, slot


def routes(topo, R, slot):
    calls = {}
    for ch in R:
        h, f = R[ch], R[[k for k in R if k != ch][0]]
        d, i1, i2, x = h["d"], h["i1"], h["i2"], h["x"]
        A, B, D, F = slot[i1], slot[i2], slot[d], slot[f["d"]]
        out = topo.mask(d, f["d"])
        stay = topo.mask(d, i1) & ~out
        calls[d] = [("c", D, 1, [f["d"]], out), ("p", D, 1, [f["d"]], out),
                    ("c", D, 1, [i1, i2], stay), ("p", D, 1, [i1, i2], stay),
                    ("c", F, 1, [i1, i2], out), ("p", F, 1, [i1, i2], stay),
                    ("c", B, 1, [f["d"]], out)]
        calls[i1] = [("c", A, 1, [h["r1"]], out), ("p", A, 1, [x, d, i2], stay), ("c", A, 1, [d, i2], out | stay),
                     ("c", A, 1, [x], stay)]
        calls[i2] = [("c", B, 1, [h["r2"]], out), ("p", B, 1, [x, d, i1], stay), ("c", B, 1, [d, i1], out | stay)]
        calls[h["r1"]] = [("c", A, 1, [f["i1"], f["d"]], out)]
        calls[h["r2"]] = [("c", B, 1, [f["i2"], f["i1"]], out)]
        calls[x] = [("p", A, 2, [f["i1"], f["i2"], f["d"]], out), ("c", A, 1, [f["i2"]], out)]
    return calls


def rank_program(g, core, T, topo):
    S = T.sem
    rank = T.rank_of(core)
    mychip = topo.chip(core)
    R, slot = roles(T, topo)
    calls = routes(topo, R, slot)
    lands = {}
    for cl in calls.values():
        for k, s, n, dsts, m in cl:
            if core in dsts:
                for i in range(n):
                    lands[k, s + i] = (S["%s%d" % (k, s)], bits(m))

    def send():
        for k, s, n, dsts, m in calls[core]:
            if rank is None or s != slot[core]:
                for sem, cnt in [lands[k, s + i] for i in range(n)]:
                    g.wait_ge(sem, cnt)
            view = T.kc[:, 128 * s:128 * (s + n)].bitcast(dt.uint8) if k == "c" else T.kp[:, 128 * s:128 * (s + n)]
            ids = []
            for c in dsts:
                rid, pid, _ = topo.addr(c)
                ids.append(DstId(rid=rid, pnc=pid))
            g.remote_dma_fused([RemoteDMATransfer(dst_ids=ids, dma_engine_mask=m, remote_sem=S["%s%d" % (k, s)],
                                                  srcs=[view], dsts=[view] * len(ids))], local_sem=S.sent)
        g.wait_ge(S.sent, sum(bits(c[4]) for c in calls[core]))

    if rank is None:
        if core in calls:
            send()
        return

    v, sc, te, sy = g.vector, g.scalar, g.tensor, g.sync
    mult, add = AluOpType.mult, AluOpType.add
    Copy = ActivationFunctionType.Copy
    K = 0.019
    me = slot[core]

    sy.dma_start(T.xks[:], T.xk[:]).then_inc(S.l_xk, 16)
    sc.dma_start(T.wks[:, 0:1024], T.wk[:, 0:1024]).then_inc(S.l_w01, 16)
    sy.dma_start(T.sns[:], T.sn[:]).then_inc(S.l_sn, 16)
    sy.dma_start(T.css[:], T.cs[:]).then_inc(S.l_cs, 16)
    sc.dma_start(T.wks[:, 1024:1536], T.wk[:, 1024:1536]).then_inc(S.l_w2, 16)
    sy.dma_start(T.wks[:, 1536:2048], T.wk[:, 1536:2048]).then_inc(S.l_w3, 16)
    sy.dma_start(T.xqs[:], T.xq[:]).then_inc(S.l_xq, 16)

    def zb(i):
        return T.ps[:, 512 * i:512 * i + 128]

    def qw(i):
        a = 128 * i
        v.wait_ge((S.l_w01, S.l_w01, S.l_w2, S.l_w3)[i], 16)
        v.quantize_mx(T.wc[:, a:a + 128], T.wp[:, a:a + 128], T.wks[:, 4 * a:4 * a + 512]).then_inc(S["qw%d" % i], 1)

    te.wait_ge(S.qx, 1)
    for i in range(4):
        a = 128 * i
        te.wait_ge(S["qw%d" % i], 1)
        te.matmul_mx(zb(i), T.wc[:, a:a + 128], T.wp[:, a:a + 128], T.xc[:], T.xp[:], True, True).then_inc(S["z%d" % i], 1)

    def scan(out, z, z0, data, a, b, done):
        v.tensor_tensor_scan(out[:, a:b], z[:, a - z0:b - z0], data[:, a:b], 0.0, mult, add).then_inc(done, 1)

    v.memset(T.za[:], 0.0).then_inc(S.zero, 1)
    v.memset(T.zb[:], 0.0).then_inc(S.zero, 1)
    v.wait_ge(S.l_xk, 16)
    v.quantize_mx(T.xc[:], T.xp[:], T.xks[:]).then_inc(S.qx, 1)
    qw(0)
    qw(1)
    qw(2)
    v.wait_ge(S.z0, 1)
    v.wait_ge(S.l_sn, 16)
    v.tensor_tensor(T.da[:, 257:512:2], zb(0), T.sns[:], mult).then_inc(S.da1, 1)
    v.wait_ge(S.l_cs, 16)
    v.tensor_tensor(T.da[:, 1:256:2], zb(0), T.css[:], mult).then_inc(S.da0, 1)
    qw(3)
    v.wait_ge(S.z2, 1)
    v.tensor_tensor(T.db[:, 1:256:2], zb(2), T.css[:], mult).then_inc(S.db0, 1)
    v.tensor_tensor(T.db[:, 257:512:2], zb(2), T.sns[:], mult).then_inc(S.db1, 1)
    v.wait_ge(S.zc1, 1)
    v.wait_ge(S.da0, 2)
    scan(T.ra, T.za, 0, T.da, 0, 256, S.sa0)
    v.wait_ge(S.da1, 2)
    scan(T.ra, T.za, 256, T.da, 256, 512, S.sa1)
    v.wait_ge(S.zc3, 1)
    v.wait_ge(S.db0, 2)
    scan(T.rb, T.zb, 0, T.db, 0, 256, S.sb0)
    v.wait_ge(S.db1, 2)
    scan(T.rb, T.zb, 256, T.db, 256, 384, S.sb1)
    scan(T.rb, T.zb, 256, T.db, 384, 512, S.sb2)
    v.wait_ge(S.sb2, 1)
    v.tensor_scalar(T.kt[:, 259:512:4], T.rb[:, 385:512:2], K, None, mult).then_inc(S.tk, 1)
    v.wait_ge(S.tk, 5)
    v.quantize_mx(T.kc[:, 128 * me:128 * me + 128], T.kp[:, 128 * me:128 * me + 128], T.kt[:]).then_inc(S.qk, 1)
    v.wait_ge(S.l_xq, 16)
    v.quantize_mx(T.qc[:], T.qp[:], T.xqs[:]).then_inc(S.qq, 1)

    sc.wait_ge(S.l_sn, 16)
    sc.activation(T.da[:, 0:256:2], T.sns[:], Copy, scale=-1.0).then_inc(S.da0, 1)
    sc.activation(T.db[:, 0:256:2], T.sns[:], Copy, scale=-1.0).then_inc(S.db0, 1)
    sc.wait_ge(S.zero, 2)
    sc.wait_ge(S.z1, 1)
    sc.activation(T.za[:, 1:256:2], zb(1), Copy).then_inc(S.zc1, 1)
    sc.wait_ge(S.l_cs, 16)
    sc.activation(T.db[:, 256:512:2], T.css[:], Copy).then_inc(S.db1, 1)
    sc.activation(T.da[:, 256:512:2], T.css[:], Copy).then_inc(S.da1, 1)
    sc.wait_ge(S.z3, 1)
    sc.activation(T.zb[:, 1:256:2], zb(3), Copy).then_inc(S.zc3, 1)
    for b, (done, r) in enumerate(((S.sa0, T.ra[:, 1:256:2]), (S.sa1, T.ra[:, 257:512:2]), (S.sb0, T.rb[:, 1:256:2]))):
        sc.wait_ge(done, 1)
        sc.activation(T.kt[:, b:512:4], r, Copy, scale=K).then_inc(S.tk, 1)
    sc.wait_ge(S.sb1, 1)
    sc.activation(T.kt[:, 3:256:4], T.rb[:, 257:384:2], Copy, scale=K).then_inc(S.tk, 1)

    g.wait_ge(S.qk, 1)
    send()

    h, f = R[mychip], R[[k for k in R if k != mychip][0]]
    order = [core] + {h["d"]: [h["i1"], f["d"], h["i2"], f["i1"], f["i2"]],
                      h["i1"]: [h["i2"], h["d"], f["d"], f["i1"], f["i2"]],
                      h["i2"]: [h["i1"], h["d"], f["d"], f["i2"], f["i1"]]}[core]
    for i, c in enumerate(order):
        y0 = NQ * list(T.cores).index(c)
        s = slot[c]
        for sem, cnt in ([(S.qk, 1), (S.qq, 1)] if c == core else [lands["p", s], lands["c", s]]):
            te.wait_ge(sem, cnt)
        for n, (a, b) in enumerate(CUTS):
            bank = 512 * ((4 + 2 * i + n) % 8)
            acc = T.ps[:, bank:bank + b - a]
            if i >= 4:
                te.wait_ge(S["e%d_%d" % (i - 4, n)], 1)
            te.matmul_mx(acc, T.kc[:, 128 * s:128 * s + 128], T.kp[:, 128 * s:128 * s + 128],
                         T.qc[:, a:b], T.qp[:, a:b], True, True).then_inc(S["p%d_%d" % (i, n)], 1)
            if n == 0:
                v.wait_ge(S["p%d_0" % i], 1)
                v.tensor_copy(T.ys[:, y0 + a:y0 + b], acc).then_inc(S["e%d_0" % i], 1)
            else:
                sc.wait_ge(S["p%d_1" % i], 1)
                sc.activation(T.ys[:, y0 + a:y0 + b], acc, Copy).then_inc(S["e%d_1" % i], 1)
        sy.wait_ge(S["e%d_0" % i], 1)
        sy.wait_ge(S["e%d_1" % i], 1)
        sy.dma_start(T.y[:, y0:y0 + NQ], T.ys[:, y0:y0 + NQ]).then_inc(S.st, 16)
    sy.wait_ge(S.st, 16 * N)
